import numpy as np
import ml_dtypes


def mxq(x, axis, fmt="e4m3"):
    dtype, down = {"e4m3": (ml_dtypes.float8_e4m3fn, 7), "e5m2": (ml_dtypes.float8_e5m2, 14)}[fmt]
    v = np.moveaxis(np.asarray(x, np.float32).astype(ml_dtypes.bfloat16).astype(np.float64), axis, -1)
    blocks = v.reshape(v.shape[:-1] + (-1, 32))
    amax = np.abs(blocks).max(-1, keepdims=True)
    byte = np.maximum(np.where(amax > 0, np.frexp(amax)[1] - 1 + 127, 0) - down, 1)
    scale = np.exp2(byte - 127.0)
    codes = (blocks / scale).astype(np.float32).astype(dtype).astype(np.float64)
    return np.moveaxis((codes * scale).reshape(v.shape), -1, axis)


WIDE = False


def mx_kscale(k):
    if not WIDE:
        return np.ones(k)
    levels = np.array([10, -10, 5, -5, 0])
    if k % 512:
        return np.exp2(np.random.permutation(np.resize(levels, k // 32))).repeat(32)
    a = np.empty((k // 512, 16))
    for p in range(k // 512):
        a[p, :8] = np.random.permutation(np.resize(levels, 8))
        for g in range(8):
            far = levels[np.abs(levels - a[p, g]) >= 10]
            a[p, g + 8] = far[np.random.randint(len(far))]
    return np.exp2(a.ravel()).repeat(32)


def f64(x):
    return np.asarray(x).astype(np.float64)


def striped(idx):
    return np.tile(idx.reshape(-1, 16).T, (8, 1)).astype(np.uint16)


def unstriped(offs):
    return offs[:16].T.reshape(-1).astype(np.int64)


def silu(v):
    return v / (1.0 + np.exp(-np.maximum(v, -700.0)))


K, T, H, N = 512, 512, 1024, 128


def setup_inputs():
    n = np.random.standard_normal
    s = mx_kscale(K)[:, None]
    u = mx_kscale(H)
    idx = np.random.permutation(H)
    v = np.empty(H)
    v[idx] = u
    return {
        "xT": (n((K, T)) * s).astype(np.float32),
        "w1": (n((K, H)) / np.sqrt(K) / s * v).astype(np.float32),
        "w2": (n((H, N)) / np.sqrt(H) / u[:, None]).astype(np.float32),
        "offs": striped(idx),
    }


def reference(xT, w1, w2, offs):
    idx = unstriped(offs)
    h = silu(mxq(f64(w1), 0, "e4m3").T @ mxq(f64(xT), 0, "e4m3"))
    return mxq(f64(w2), 0, "e4m3").T @ mxq(h[idx], 0, "e4m3")

@@ -1,0 +1,182 @@
+from contextlib import ExitStack
+
+import concourse.mybir as mybir
+from concourse.masks import make_identity
+
+FLOPS = 671088640
+
+F32 = mybir.dt.float32
+BF16 = mybir.dt.bfloat16
+U32 = mybir.dt.uint32
+U16 = mybir.dt.uint16
+U8 = mybir.dt.uint8
+FP8X4 = mybir.dt.float8_e4m3fn_x4
+COPY = mybir.ActivationFunctionType.Copy
+SILU = mybir.ActivationFunctionType.Silu
+MULT = mybir.AluOpType.mult
+ADD = mybir.AluOpType.add
+
+P = 128
+H = 1024
+T = 512
+N = 128
+CH = 256
+TB = 256
+
+
+def tile_picked_shuffle_mlp_silu_perm_l_kernel(tc, xT, w1, w2, offs, out):
+    nc = tc.nc
+    with ExitStack() as ctx:
+        keep = ctx.enter_context(tc.tile_pool(name="keep", bufs=1))
+        banks = ctx.enter_context(tc.psum_pool(name="banks", bufs=1))
+
+        offsets = keep.tile([P, H // 16], U16, name="offsets")
+        x_view = xT.rearrange("(p j) t -> p j t", j=4)
+        w1_view = w1.rearrange("(p j) c -> p j c", j=4)
+
+        x_raw = [keep.tile([P, 4, TB], F32, name=f"x_raw{b}") for b in range(2)]
+        w1_raw = [keep.tile([P, 4, CH], F32, name=f"w1_raw{c}") for c in range(H // CH)]
+        w2_raw = keep.tile([P, 2, 4, N], F32, name="w2_raw")
+
+        nc.sync.dma_start(x_raw[0][:], x_view[:, :, 0:TB])
+        nc.sync.dma_start(x_raw[1][:], x_view[:, :, TB : 2 * TB])
+        for c in range(H // CH):
+            nc.sync.dma_start(w1_raw[c][:], w1_view[:, :, c * CH : (c + 1) * CH])
+        nc.sync.dma_start(offsets[:], offs)
+        nc.sync.dma_start(w2_raw[:], w2.rearrange("(g p j) n -> p g j n", g=2, j=4))
+
+        warm = keep.tile([P, 1], F32, name="warm")
+        warm2 = keep.tile([P, 1], F32, name="warm2")
+        nc.gpsimd.memset(warm[:], 0.0)
+        nc.scalar.activation(warm2[:], warm[:], SILU)
+        ident = keep.tile([P, P], F32, name="ident")
+        make_identity(nc, ident[:])
+
+        def gp_copy(out, in_):
+            nc.gpsimd.tensor_scalar(out=out, in0=in_, scalar1=1.0, scalar2=0.0, op0=MULT, op1=ADD)
+
+        V, S, G = nc.vector.tensor_copy, nc.scalar.copy, gp_copy
+
+        def bank(index, shape):
+            return banks.tile(shape, F32, name=f"bank{index}", tag=f"bank{index}")
+
+        def quant(dst_name, bf, width):
+            codes = keep.tile([P, width], U32, name=dst_name + "_codes", align_bytes=64)
+            scales = keep.tile([P, width], U8, name=dst_name + "_scales", align_bytes=64)
+            nc.vector.quantize_mx(out=codes[:].bitcast(FP8X4), scales=scales[:], in_=bf[:])
+            return codes, scales
+
+        def cast(dst_name, raw, width, parts):
+            bf = keep.tile([P, 4 * width], BF16, name=dst_name + "_bf", tag=dst_name + "_bf", align_bytes=64)
+            c0 = 0
+            for copy, w in parts:
+                copy(
+                    bf[:, 4 * c0 : 4 * (c0 + w)].rearrange("p (c i j) -> p c j i", i=4, j=4),
+                    raw[:, :, c0 : c0 + w].rearrange("p j (c i) -> p c j i", i=4),
+                )
+                c0 += w
+            return bf
+
+        h = [keep.tile([P, 2 * H], BF16, name=f"h{b}", align_bytes=64) for b in range(2)]
+
+        def layer1(b, c, xq, wq):
+            ps = bank(4 * b + c, [P, 2, CH])
+            for e in range(2):
+                cols = slice(e * P, (e + 1) * P)
+                nc.tensor.matmul_mx(
+                    out=ps[:, e, :],
+                    lhsT=xq[0][:, cols].bitcast(FP8X4),
+                    lhsT_scale=xq[1][:, cols],
+                    rhs=wq[0][:].bitcast(FP8X4),
+                    rhs_scale=wq[1][:],
+                    start=True,
+                    stop=True,
+                )
+            nc.scalar.activation(
+                h[b][:, 2 * c * CH : 2 * (c + 1) * CH].rearrange("p (c e) -> p c e", e=2),
+                ps[:].rearrange("p e c -> p c e"),
+                SILU,
+            )
+
+        xa_bf = cast("xa", x_raw[0], TB, [(V, 256)])
+        xb_bf = cast("xb", x_raw[1], TB, [(G, 256)])
+        xq = [quant("xa", xa_bf, TB), None]
+        parts = [[(V, 256)], [(V, 256)], [(V, 256)], [(V, 128), (S, 128)]]
+        w1q = []
+        for c in range(4):
+            w1_bf = cast(f"w1_{c}", w1_raw[c], CH, parts[c])
+            if c == 0:
+                xq[1] = quant("xb", xb_bf, TB)
+            w1q.append(quant(f"w1_{c}", w1_bf, CH))
+            layer1(0, c, xq[0], w1q[c])
+            if c > 0:
+                layer1(1, c - 1, xq[1], w1q[c - 1])
+        layer1(1, 3, xq[1], w1q[3])
+
+        w2_bf = keep.tile([P, 8 * N], BF16, name="w2_bf", align_bytes=64)
+        gp_copy(
+            w2_bf[:].rearrange("p (g n j) -> p g n j", g=2, j=4),
+            w2_raw[:].rearrange("p g j n -> p g n j"),
+        )
+
+        def gather(b, g):
+            tag = f"gt{b}{g}"
+            gt = keep.tile([P, 1024], BF16, name=f"gt{b}{g}", tag=tag, align_bytes=64)
+            nc.vector.tensor_copy(
+                out=gt[:].bitcast(U32).rearrange("p (t m) -> p m t", t=4),
+                in_=h[b][:].bitcast(U32).indirect(offsets[:, 32 * g : 32 * (g + 1)]),
+            )
+            return gt
+
+        def turn(gt, b):
+            pt = bank(b, [P, 4, P])
+            for t in range(4):
+                nc.tensor.transpose(pt[:, t, :], gt[:].bitcast(F32)[:, t * P : (t + 1) * P], ident[:])
+            return pt
+
+        def evac(name, pt, parts):
+            hb = keep.tile([P, 1024], BF16, name=name, align_bytes=64)
+            for copy, e0, e1 in parts:
+                copy(
+                    hb[:].rearrange("p (e q t) -> p e q t", e=2, t=4)[:, e0:e1],
+                    pt[:].bitcast(BF16).rearrange("p t (q e) -> p e q t", e=2)[:, e0:e1],
+                )
+            return hb
+
+        def layer2(out_cols, g, hq):
+            nc.tensor.matmul_mx(
+                out=out_cols,
+                lhsT=w2q[0][:, g * N : (g + 1) * N].bitcast(FP8X4),
+                lhsT_scale=w2q[1][:, g * N : (g + 1) * N],
+                rhs=hq[0][:].bitcast(FP8X4),
+                rhs_scale=hq[1][:],
+                start=(g == 0),
+                stop=(g == 1),
+            )
+
+        def leave(b, acc):
+            res = keep.tile([P, TB], F32, name=f"res{b}")
+            nc.scalar.copy(res[:], acc[:])
+            nc.sync.dma_start(out[:, b * TB : (b + 1) * TB], res[:])
+
+        pa0 = turn(gather(0, 0), 0)
+        pa1 = turn(gather(0, 1), 1)
+        ha0 = evac("ha0", pa0, [(S, 0, 2)])
+        w2q = quant("w2", w2_bf, 2 * N)
+        ha1 = evac("ha1", pa1, [(S, 0, 2)])
+        pb0 = turn(gather(1, 0), 4)
+        qa0 = quant("ha0q", ha0, TB)
+        acc_a = bank(2, [P, TB])
+        layer2(acc_a[:], 0, qa0)
+        hb0 = evac("hb0", pb0, [(S, 0, 2)])
+        pb1 = turn(gather(1, 1), 5)
+        qa1 = quant("ha1q", ha1, TB)
+        layer2(acc_a[:], 1, qa1)
+        leave(0, acc_a)
+        qb0 = quant("hb0q", hb0, TB)
+        acc_b = bank(3, [P, TB])
+        layer2(acc_b[:], 0, qb0)
+        hb1 = evac("hb1", pb1, [(S, 0, 2)])
+        qb1 = quant("hb1q", hb1, TB)
+        layer2(acc_b[:], 1, qb1)
+        leave(1, acc_b)

@@ -20,7 +20,7 @@ P = 128
 H = 1024
 T = 512
 N = 128
-CH = 256
+CHUNKS = ((0, 256), (256, 256), (512, 256), (768, 256))
 TB = 256
 
 
@@ -35,13 +35,13 @@ def tile_picked_shuffle_mlp_silu_perm_l_kernel(tc, xT, w1, w2, offs, out):
         w1_view = w1.rearrange("(p j) c -> p j c", j=4)
 
         x_raw = [keep.tile([P, 4, TB], F32, name=f"x_raw{b}") for b in range(2)]
-        w1_raw = [keep.tile([P, 4, CH], F32, name=f"w1_raw{c}") for c in range(H // CH)]
+        w1_raw = [keep.tile([P, 4, w], F32, name=f"w1_raw{c0}") for c0, w in CHUNKS]
         w2_raw = keep.tile([P, 2, 4, N], F32, name="w2_raw")
 
         nc.sync.dma_start(x_raw[0][:], x_view[:, :, 0:TB])
+        for raw, (c0, w) in zip(w1_raw, CHUNKS):
+            nc.sync.dma_start(raw[:], w1_view[:, :, c0 : c0 + w])
         nc.sync.dma_start(x_raw[1][:], x_view[:, :, TB : 2 * TB])
-        for c in range(H // CH):
-            nc.sync.dma_start(w1_raw[c][:], w1_view[:, :, c * CH : (c + 1) * CH])
         nc.sync.dma_start(offsets[:], offs)
         nc.sync.dma_start(w2_raw[:], w2.rearrange("(g p j) n -> p g j n", g=2, j=4))
 
@@ -79,48 +79,51 @@ def tile_picked_shuffle_mlp_silu_perm_l_kernel(tc, xT, w1, w2, offs, out):
 
         h = [keep.tile([P, 2 * H], BF16, name=f"h{b}", align_bytes=64) for b in range(2)]
 
-        def layer1(b, c, xq, wq):
-            ps = bank(4 * b + c, [P, 2, CH])
+        w1_codes = keep.tile([P, H], U32, name="w1_codes", align_bytes=64)
+        w1_scales = keep.tile([P, H], U8, name="w1_scales", align_bytes=64)
+
+        def quant_w1(bf, c0, w):
+            cols = slice(c0, c0 + w)
+            nc.vector.quantize_mx(out=w1_codes[:, cols].bitcast(FP8X4), scales=w1_scales[:, cols], in_=bf[:])
+
+        def layer1(b, ps, c0, w, xq):
+            ch = slice(c0, c0 + w)
             for e in range(2):
                 cols = slice(e * P, (e + 1) * P)
                 nc.tensor.matmul_mx(
                     out=ps[:, e, :],
                     lhsT=xq[0][:, cols].bitcast(FP8X4),
                     lhsT_scale=xq[1][:, cols],
-                    rhs=wq[0][:].bitcast(FP8X4),
-                    rhs_scale=wq[1][:],
+                    rhs=w1_codes[:, ch].bitcast(FP8X4),
+                    rhs_scale=w1_scales[:, ch],
                     start=True,
                     stop=True,
                 )
             nc.scalar.activation(
-                h[b][:, 2 * c * CH : 2 * (c + 1) * CH].rearrange("p (c e) -> p c e", e=2),
+                h[b][:, 2 * c0 : 2 * (c0 + w)].rearrange("p (c e) -> p c e", e=2),
                 ps[:].rearrange("p e c -> p c e"),
                 SILU,
             )
 
-        xa_bf = cast("xa", x_raw[0], TB, [(V, 256)])
-        xb_bf = cast("xb", x_raw[1], TB, [(G, 256)])
-        xq = [quant("xa", xa_bf, TB), None]
-        parts = [[(V, 256)], [(V, 256)], [(V, 256)], [(V, 128), (S, 128)]]
-        w1q = []
+        xa = quant("xa", cast("xa", x_raw[0], TB, [(V, 128), (S, 128)]), TB)
+        w1_parts = [[(V, 128), (S, 128)], [(V, 256)], [(V, 256)], [(V, 256)]]
+        for i, (c0, w) in enumerate(CHUNKS):
+            quant_w1(cast(f"w1_{i}", w1_raw[i], w, w1_parts[i]), c0, w)
+            layer1(0, bank(i, [P, 2, w]), c0, w, xa)
+        xb = quant("xb", cast("xb", x_raw[1], TB, [(V, 256)]), TB)
         for c in range(4):
-            w1_bf = cast(f"w1_{c}", w1_raw[c], CH, parts[c])
-            if c == 0:
-                xq[1] = quant("xb", xb_bf, TB)
-            w1q.append(quant(f"w1_{c}", w1_bf, CH))
-            layer1(0, c, xq[0], w1q[c])
-            if c > 0:
-                layer1(1, c - 1, xq[1], w1q[c - 1])
-        layer1(1, 3, xq[1], w1q[3])
+            layer1(1, bank([5, 6, 7, 0][c], [P, 2, 256]), 256 * c, 256, xb)
 
         w2_bf = keep.tile([P, 8 * N], BF16, name="w2_bf", align_bytes=64)
-        gp_copy(
-            w2_bf[:].rearrange("p (g n j) -> p g n j", g=2, j=4),
-            w2_raw[:].rearrange("p g j n -> p g n j"),
-        )
+
+        def cast_w2(copy):
+            copy(
+                w2_bf[:].rearrange("p (g n j) -> p g n j", g=2, j=4),
+                w2_raw[:].rearrange("p g j n -> p g n j"),
+            )
 
         def gather(b, g):
-            tag = f"gt{b}{g}"
+            tag = "xb_bf" if (b, g) == (0, 0) else f"gt{b}{g}"
             gt = keep.tile([P, 1024], BF16, name=f"gt{b}{g}", tag=tag, align_bytes=64)
             nc.vector.tensor_copy(
                 out=gt[:].bitcast(U32).rearrange("p (t m) -> p m t", t=4),
@@ -159,24 +162,29 @@ def tile_picked_shuffle_mlp_silu_perm_l_kernel(tc, xT, w1, w2, offs, out):
             nc.scalar.copy(res[:], acc[:])
             nc.sync.dma_start(out[:, b * TB : (b + 1) * TB], res[:])
 
-        pa0 = turn(gather(0, 0), 0)
-        pa1 = turn(gather(0, 1), 1)
+        cast_w2(G)
+        pa0 = turn(gather(0, 0), 6)
+        pa1 = turn(gather(0, 1), 7)
         ha0 = evac("ha0", pa0, [(S, 0, 2)])
         w2q = quant("w2", w2_bf, 2 * N)
         ha1 = evac("ha1", pa1, [(S, 0, 2)])
-        pb0 = turn(gather(1, 0), 4)
-        qa0 = quant("ha0q", ha0, TB)
+        pb0 = turn(gather(1, 0), 1)
+        qa0 = quant("ha0q", ha0[:], TB)
         acc_a = bank(2, [P, TB])
         layer2(acc_a[:], 0, qa0)
         hb0 = evac("hb0", pb0, [(S, 0, 2)])
-        pb1 = turn(gather(1, 1), 5)
-        qa1 = quant("ha1q", ha1, TB)
+        pb1 = turn(gather(1, 1), 3)
+        qa1 = quant("ha1q", ha1[:], TB)
         layer2(acc_a[:], 1, qa1)
         leave(0, acc_a)
-        qb0 = quant("hb0q", hb0, TB)
-        acc_b = bank(3, [P, TB])
-        layer2(acc_b[:], 0, qb0)
-        hb1 = evac("hb1", pb1, [(S, 0, 2)])
-        qb1 = quant("hb1q", hb1, TB)
-        layer2(acc_b[:], 1, qb1)
-        leave(1, acc_b)
+        qb0 = quant("hb0q", hb0[:], TB)
+        hb1 = evac("hb1", pb1, [(S, 0, 1), (S, 1, 2)])
+        for e in range(2):
+            cols = slice(e * P, (e + 1) * P)
+            qb1 = quant(f"hb1q{e}", hb1[:, 512 * e : 512 * (e + 1)], P)
+            acc_b = bank(4 if e else 5, [P, P])
+            layer2(acc_b[:], 0, [plane[:, cols] for plane in qb0])
+            layer2(acc_b[:], 1, qb1)
+            res = keep.tile([P, P], F32, name=f"res_b{e}")
+            nc.scalar.copy(res[:], acc_b[:])
+            nc.sync.dma_start(out[:, TB + e * P : TB + (e + 1) * P], res[:])

@@ -11,7 +11,6 @@ U32 = mybir.dt.uint32
 U16 = mybir.dt.uint16
 U8 = mybir.dt.uint8
 FP8X4 = mybir.dt.float8_e4m3fn_x4
-COPY = mybir.ActivationFunctionType.Copy
 SILU = mybir.ActivationFunctionType.Silu
 MULT = mybir.AluOpType.mult
 ADD = mybir.AluOpType.add
@@ -20,7 +19,6 @@ P = 128
 H = 1024
 T = 512
 N = 128
-CHUNKS = ((0, 256), (256, 256), (512, 256), (768, 256))
 TB = 256
 
 
@@ -33,18 +31,31 @@ def tile_picked_shuffle_mlp_silu_perm_l_kernel(tc, xT, w1, w2, offs, out):
         offsets = keep.tile([P, H // 16], U16, name="offsets")
         x_view = xT.rearrange("(p j) t -> p j t", j=4)
         w1_view = w1.rearrange("(p j) c -> p j c", j=4)
-
-        x_raw = [keep.tile([P, 4, TB], F32, name=f"x_raw{b}") for b in range(2)]
-        w1_raw = [keep.tile([P, 4, w], F32, name=f"w1_raw{c0}") for c0, w in CHUNKS]
+        x_raw = {}
+        w1_raw = {}
         w2_raw = keep.tile([P, 2, 4, N], F32, name="w2_raw")
 
-        nc.sync.dma_start(x_raw[0][:], x_view[:, :, 0:TB])
-        for raw, (c0, w) in zip(w1_raw, CHUNKS):
-            nc.sync.dma_start(raw[:], w1_view[:, :, c0 : c0 + w])
-        nc.sync.dma_start(x_raw[1][:], x_view[:, :, TB : 2 * TB])
-        nc.sync.dma_start(offsets[:], offs)
-        nc.sync.dma_start(w2_raw[:], w2.rearrange("(g p j) n -> p g j n", g=2, j=4))
+        def load_x(t0, w):
+            x_raw[t0] = keep.tile([P, 4, w], F32, name=f"x_raw{t0}" if w < T else "x_raw")
+            nc.sync.dma_start(x_raw[t0][:], x_view[:, :, t0 : t0 + w])
 
+        def load_w1(c0, w):
+            w1_raw[c0] = keep.tile([P, 4, w], F32, name=f"w1_raw{c0}")
+            nc.sync.dma_start(w1_raw[c0][:], w1_view[:, :, c0 : c0 + w])
+
+        def load_offs():
+            nc.sync.dma_start(offsets[:], offs)
+
+        def load_w2():
+            nc.sync.dma_start(w2_raw[:], w2.rearrange("(g p j) n -> p g j n", g=2, j=4))
+
+        load_x(0, 256)
+        load_w1(0, 512)
+        load_w1(512, 256)
+        load_w1(768, 256)
+        load_x(256, 256)
+        load_offs()
+        load_w2()
         warm = keep.tile([P, 1], F32, name="warm")
         warm2 = keep.tile([P, 1], F32, name="warm2")
         nc.gpsimd.memset(warm[:], 0.0)
@@ -52,48 +63,55 @@ def tile_picked_shuffle_mlp_silu_perm_l_kernel(tc, xT, w1, w2, offs, out):
         ident = keep.tile([P, P], F32, name="ident")
         make_identity(nc, ident[:])
 
-        def gp_copy(out, in_):
-            nc.gpsimd.tensor_scalar(out=out, in0=in_, scalar1=1.0, scalar2=0.0, op0=MULT, op1=ADD)
+        V, S = nc.vector.tensor_copy, nc.scalar.copy
 
-        V, S, G = nc.vector.tensor_copy, nc.scalar.copy, gp_copy
+        def G(out, in_):
+            nc.gpsimd.tensor_scalar(out=out, in0=in_, scalar1=1.0, scalar2=0.0, op0=MULT, op1=ADD)
 
         def bank(index, shape):
             return banks.tile(shape, F32, name=f"bank{index}", tag=f"bank{index}")
 
-        def quant(dst_name, bf, width):
-            codes = keep.tile([P, width], U32, name=dst_name + "_codes", align_bytes=64)
-            scales = keep.tile([P, width], U8, name=dst_name + "_scales", align_bytes=64)
-            nc.vector.quantize_mx(out=codes[:].bitcast(FP8X4), scales=scales[:], in_=bf[:])
-            return codes, scales
-
-        def cast(dst_name, raw, width, parts):
-            bf = keep.tile([P, 4 * width], BF16, name=dst_name + "_bf", tag=dst_name + "_bf", align_bytes=64)
-            c0 = 0
-            for copy, w in parts:
-                copy(
-                    bf[:, 4 * c0 : 4 * (c0 + w)].rearrange("p (c i j) -> p c j i", i=4, j=4),
-                    raw[:, :, c0 : c0 + w].rearrange("p j (c i) -> p c j i", i=4),
-                )
-                c0 += w
-            return bf
-
-        h = [keep.tile([P, 2 * H], BF16, name=f"h{b}", align_bytes=64) for b in range(2)]
-
+        x_bf = [keep.tile([P, 4 * TB], BF16, name=f"x_bf{b}", tag=f"x_bf{b}", align_bytes=64) for b in range(2)]
+        x_codes = [keep.tile([P, TB], U32, name=f"x_codes{b}", align_bytes=64) for b in range(2)]
+        x_scales = [keep.tile([P, TB], U8, name=f"x_scales{b}", align_bytes=64) for b in range(2)]
         w1_codes = keep.tile([P, H], U32, name="w1_codes", align_bytes=64)
         w1_scales = keep.tile([P, H], U8, name="w1_scales", align_bytes=64)
+        w1_bf = keep.tile([P, 4 * H], BF16, name="w1_bf", align_bytes=64)
+        w2_bf = keep.tile([P, 8 * N], BF16, name="w2_bf", align_bytes=64)
+        w2_codes = keep.tile([P, 2 * N], U32, name="w2_codes", align_bytes=64)
+        w2_scales = keep.tile([P, 2 * N], U8, name="w2_scales", align_bytes=64)
+        h = [keep.tile([P, 2 * H], BF16, name=f"h{b}", align_bytes=64) for b in range(2)]
 
-        def quant_w1(bf, c0, w):
-            cols = slice(c0, c0 + w)
-            nc.vector.quantize_mx(out=w1_codes[:, cols].bitcast(FP8X4), scales=w1_scales[:, cols], in_=bf[:])
+        def interleave(copy, dst, src):
+            copy(dst.rearrange("p (c i j) -> p c j i", i=4, j=4), src.rearrange("p j (c i) -> p c j i", i=4))
 
-        def layer1(b, ps, c0, w, xq):
+        def quant(codes, scales, bf):
+            nc.vector.quantize_mx(out=codes.bitcast(FP8X4), scales=scales, in_=bf)
+
+        def cast_x(copy, b, raw, r0, c0, w):
+            interleave(copy, x_bf[b][:, 4 * c0 : 4 * (c0 + w)], raw[:, :, r0 : r0 + w])
+
+        def quant_x(b):
+            quant(x_codes[b][:], x_scales[b][:], x_bf[b][:])
+
+        def cast_w1(copy, raw, r0, c0, w):
+            interleave(copy, w1_bf[:, 4 * c0 : 4 * (c0 + w)], raw[:, :, r0 : r0 + w])
+
+        def quant_w1(c0, w):
+            quant(w1_codes[:, c0 : c0 + w], w1_scales[:, c0 : c0 + w], w1_bf[:, 4 * c0 : 4 * (c0 + w)])
+
+        def cast_w2(copy):
+            copy(w2_bf[:].rearrange("p (g n j) -> p g n j", g=2, j=4), w2_raw[:].rearrange("p g j n -> p g n j"))
+
+        def layer1(b, bank_index, c0, w):
+            ps = bank(bank_index, [P, 2, w])
             ch = slice(c0, c0 + w)
             for e in range(2):
                 cols = slice(e * P, (e + 1) * P)
                 nc.tensor.matmul_mx(
                     out=ps[:, e, :],
-                    lhsT=xq[0][:, cols].bitcast(FP8X4),
-                    lhsT_scale=xq[1][:, cols],
+                    lhsT=x_codes[b][:, cols].bitcast(FP8X4),
+                    lhsT_scale=x_scales[b][:, cols],
                     rhs=w1_codes[:, ch].bitcast(FP8X4),
                     rhs_scale=w1_scales[:, ch],
                     start=True,
@@ -105,86 +123,101 @@ def tile_picked_shuffle_mlp_silu_perm_l_kernel(tc, xT, w1, w2, offs, out):
                 SILU,
             )
 
-        xa = quant("xa", cast("xa", x_raw[0], TB, [(V, 128), (S, 128)]), TB)
-        w1_parts = [[(V, 128), (S, 128)], [(V, 256)], [(V, 256)], [(V, 256)]]
-        for i, (c0, w) in enumerate(CHUNKS):
-            quant_w1(cast(f"w1_{i}", w1_raw[i], w, w1_parts[i]), c0, w)
-            layer1(0, bank(i, [P, 2, w]), c0, w, xa)
-        xb = quant("xb", cast("xb", x_raw[1], TB, [(V, 256)]), TB)
-        for c in range(4):
-            layer1(1, bank([5, 6, 7, 0][c], [P, 2, 256]), 256 * c, 256, xb)
-
-        w2_bf = keep.tile([P, 8 * N], BF16, name="w2_bf", align_bytes=64)
-
-        def cast_w2(copy):
-            copy(
-                w2_bf[:].rearrange("p (g n j) -> p g n j", g=2, j=4),
-                w2_raw[:].rearrange("p g j n -> p g n j"),
-            )
-
         def gather(b, g):
-            tag = "xb_bf" if (b, g) == (0, 0) else f"gt{b}{g}"
-            gt = keep.tile([P, 1024], BF16, name=f"gt{b}{g}", tag=tag, align_bytes=64)
+            gt = keep.tile([P, 4 * P * 2], BF16, name=f"gt{b}{g}", align_bytes=64)
             nc.vector.tensor_copy(
                 out=gt[:].bitcast(U32).rearrange("p (t m) -> p m t", t=4),
                 in_=h[b][:].bitcast(U32).indirect(offsets[:, 32 * g : 32 * (g + 1)]),
             )
             return gt
 
-        def turn(gt, b):
-            pt = bank(b, [P, 4, P])
+        def turn(gt, bank_index):
+            pt = bank(bank_index, [P, 4, P])
             for t in range(4):
                 nc.tensor.transpose(pt[:, t, :], gt[:].bitcast(F32)[:, t * P : (t + 1) * P], ident[:])
             return pt
 
-        def evac(name, pt, parts):
-            hb = keep.tile([P, 1024], BF16, name=name, align_bytes=64)
-            for copy, e0, e1 in parts:
-                copy(
-                    hb[:].rearrange("p (e q t) -> p e q t", e=2, t=4)[:, e0:e1],
-                    pt[:].bitcast(BF16).rearrange("p t (q e) -> p e q t", e=2)[:, e0:e1],
-                )
-            return hb
+        h_bf = {}
+        h_codes = {}
+        h_scales = {}
 
-        def layer2(out_cols, g, hq):
+        def evac(copy, b, g, pt, e0=0, e1=2):
+            if (b, g) not in h_bf:
+                h_bf[b, g] = keep.tile([P, 4 * TB], BF16, name=f"h_bf{b}{g}", align_bytes=64)
+                h_codes[b, g] = keep.tile([P, TB], U32, name=f"h_codes{b}{g}", align_bytes=64)
+                h_scales[b, g] = keep.tile([P, TB], U8, name=f"h_scales{b}{g}", align_bytes=64)
+            copy(
+                h_bf[b, g][:].rearrange("p (e q t) -> p e q t", e=2, t=4)[:, e0:e1],
+                pt[:].bitcast(BF16).rearrange("p t (q e) -> p e q t", e=2)[:, e0:e1],
+            )
+
+        def quant_h(b, g, e0=0, e1=2):
+            cols = slice(e0 * P, e1 * P)
+            quant(h_codes[b, g][:, cols], h_scales[b, g][:, cols], h_bf[b, g][:, 4 * e0 * P : 4 * e1 * P])
+
+        def layer2(acc, b, g, e0=0, e1=2):
+            cols = slice(e0 * P, e1 * P)
             nc.tensor.matmul_mx(
-                out=out_cols,
-                lhsT=w2q[0][:, g * N : (g + 1) * N].bitcast(FP8X4),
-                lhsT_scale=w2q[1][:, g * N : (g + 1) * N],
-                rhs=hq[0][:].bitcast(FP8X4),
-                rhs_scale=hq[1][:],
+                out=acc[:],
+                lhsT=w2_codes[:, g * N : (g + 1) * N].bitcast(FP8X4),
+                lhsT_scale=w2_scales[:, g * N : (g + 1) * N],
+                rhs=h_codes[b, g][:, cols].bitcast(FP8X4),
+                rhs_scale=h_scales[b, g][:, cols],
                 start=(g == 0),
                 stop=(g == 1),
             )
 
-        def leave(b, acc):
-            res = keep.tile([P, TB], F32, name=f"res{b}")
-            nc.scalar.copy(res[:], acc[:])
-            nc.sync.dma_start(out[:, b * TB : (b + 1) * TB], res[:])
+        def leave(copy, acc, t0, w):
+            res = keep.tile([P, w], F32, name=f"res{t0}")
+            copy(res[:], acc[:])
+            nc.sync.dma_start(out[:, t0 : t0 + w], res[:])
 
+        cast_x(S, 0, x_raw[0], 0, 0, 128)
+        cast_x(V, 0, x_raw[0], 128, 128, 128)
+        quant_x(0)
+        cast_w1(V, w1_raw[0], 0, 0, 256)
+        cast_w1(S, w1_raw[0], 256, 256, 256)
+        quant_w1(0, 256)
+        layer1(0, 0, 0, 256)
+        quant_w1(256, 256)
+        layer1(0, 1, 256, 256)
+        cast_w1(S, w1_raw[512], 0, 512, 256)
+        cast_w1(V, w1_raw[768], 0, 768, 256)
+        quant_w1(512, 256)
+        layer1(0, 2, 512, 256)
+        quant_w1(768, 256)
+        layer1(0, 3, 768, 256)
+        cast_x(V, 1, x_raw[256], 0, 0, 256)
+        quant_x(1)
+        layer1(1, 4, 0, 256)
+        layer1(1, 5, 256, 256)
+        layer1(1, 6, 512, 256)
+        layer1(1, 7, 768, 256)
         cast_w2(G)
-        pa0 = turn(gather(0, 0), 6)
-        pa1 = turn(gather(0, 1), 7)
-        ha0 = evac("ha0", pa0, [(S, 0, 2)])
-        w2q = quant("w2", w2_bf, 2 * N)
-        ha1 = evac("ha1", pa1, [(S, 0, 2)])
-        pb0 = turn(gather(1, 0), 1)
-        qa0 = quant("ha0q", ha0[:], TB)
-        acc_a = bank(2, [P, TB])
-        layer2(acc_a[:], 0, qa0)
-        hb0 = evac("hb0", pb0, [(S, 0, 2)])
-        pb1 = turn(gather(1, 1), 3)
-        qa1 = quant("ha1q", ha1[:], TB)
-        layer2(acc_a[:], 1, qa1)
-        leave(0, acc_a)
-        qb0 = quant("hb0q", hb0[:], TB)
-        hb1 = evac("hb1", pb1, [(S, 0, 1), (S, 1, 2)])
-        for e in range(2):
-            cols = slice(e * P, (e + 1) * P)
-            qb1 = quant(f"hb1q{e}", hb1[:, 512 * e : 512 * (e + 1)], P)
-            acc_b = bank(4 if e else 5, [P, P])
-            layer2(acc_b[:], 0, [plane[:, cols] for plane in qb0])
-            layer2(acc_b[:], 1, qb1)
-            res = keep.tile([P, P], F32, name=f"res_b{e}")
-            nc.scalar.copy(res[:], acc_b[:])
-            nc.sync.dma_start(out[:, TB + e * P : TB + (e + 1) * P], res[:])
+        p00 = turn(gather(0, 0), 0)
+        p01 = turn(gather(0, 1), 1)
+        p10 = turn(gather(1, 0), 2)
+        quant(w2_codes[:], w2_scales[:], w2_bf[:])
+        p11 = turn(gather(1, 1), 3)
+        evac(S, 0, 0, p00, 0, 2)
+        evac(S, 0, 1, p01, 0, 2)
+        evac(S, 1, 0, p10, 0, 2)
+        evac(S, 1, 1, p11, 0, 1)
+        evac(S, 1, 1, p11, 1, 2)
+        quant_h(0, 0, 0, 2)
+        quant_h(0, 1, 0, 2)
+        quant_h(1, 0, 0, 2)
+        quant_h(1, 1, 0, 1)
+        quant_h(1, 1, 1, 2)
+        a00 = bank(4, [P, 256])
+        layer2(a00, 0, 0, 0, 2)
+        layer2(a00, 0, 1, 0, 2)
+        leave(S, a00, 0, 256)
+        a10 = bank(5, [P, 128])
+        layer2(a10, 1, 0, 0, 1)
+        layer2(a10, 1, 1, 0, 1)
+        leave(S, a10, 256, 128)
+        a11 = bank(6, [P, 128])
+        layer2(a11, 1, 0, 1, 2)
+        layer2(a11, 1, 1, 1, 2)
+        leave(S, a11, 384, 128)

from contextlib import ExitStack

import concourse.mybir as mybir
from concourse.masks import make_identity

FLOPS = 671088640

F32 = mybir.dt.float32
BF16 = mybir.dt.bfloat16
U32 = mybir.dt.uint32
U16 = mybir.dt.uint16
U8 = mybir.dt.uint8
FP8X4 = mybir.dt.float8_e4m3fn_x4
SILU = mybir.ActivationFunctionType.Silu
MULT = mybir.AluOpType.mult
ADD = mybir.AluOpType.add

P = 128
H = 1024
T = 512
N = 128
TB = 256


def tile_picked_shuffle_mlp_silu_perm_l_kernel(tc, xT, w1, w2, offs, out):
    nc = tc.nc
    with ExitStack() as ctx:
        keep = ctx.enter_context(tc.tile_pool(name="keep", bufs=1))
        banks = ctx.enter_context(tc.psum_pool(name="banks", bufs=1))

        offsets = keep.tile([P, H // 16], U16, name="offsets")
        x_view = xT.rearrange("(p j) t -> p j t", j=4)
        w1_view = w1.rearrange("(p j) c -> p j c", j=4)
        x_raw = {}
        w1_raw = {}
        w2_raw = keep.tile([P, 2, 4, N], F32, name="w2_raw")

        def load_x(t0, w):
            x_raw[t0] = keep.tile([P, 4, w], F32, name=f"x_raw{t0}" if w < T else "x_raw")
            nc.sync.dma_start(x_raw[t0][:], x_view[:, :, t0 : t0 + w])

        def load_w1(c0, w):
            w1_raw[c0] = keep.tile([P, 4, w], F32, name=f"w1_raw{c0}")
            nc.sync.dma_start(w1_raw[c0][:], w1_view[:, :, c0 : c0 + w])

        def load_offs():
            nc.sync.dma_start(offsets[:], offs)

        def load_w2():
            nc.sync.dma_start(w2_raw[:], w2.rearrange("(g p j) n -> p g j n", g=2, j=4))

        load_x(0, 256)
        load_w1(0, 512)
        load_w1(512, 256)
        load_w1(768, 256)
        load_x(256, 256)
        load_offs()
        load_w2()
        warm = keep.tile([P, 1], F32, name="warm")
        warm2 = keep.tile([P, 1], F32, name="warm2")
        nc.gpsimd.memset(warm[:], 0.0)
        nc.scalar.activation(warm2[:], warm[:], SILU)
        ident = keep.tile([P, P], F32, name="ident")
        make_identity(nc, ident[:])

        V, S = nc.vector.tensor_copy, nc.scalar.copy

        def G(out, in_):
            nc.gpsimd.tensor_scalar(out=out, in0=in_, scalar1=1.0, scalar2=0.0, op0=MULT, op1=ADD)

        def bank(index, shape):
            return banks.tile(shape, F32, name=f"bank{index}", tag=f"bank{index}")

        x_bf = [keep.tile([P, 4 * TB], BF16, name=f"x_bf{b}", tag=f"x_bf{b}", align_bytes=64) for b in range(2)]
        x_codes = [keep.tile([P, TB], U32, name=f"x_codes{b}", align_bytes=64) for b in range(2)]
        x_scales = [keep.tile([P, TB], U8, name=f"x_scales{b}", align_bytes=64) for b in range(2)]
        w1_codes = keep.tile([P, H], U32, name="w1_codes", align_bytes=64)
        w1_scales = keep.tile([P, H], U8, name="w1_scales", align_bytes=64)
        w1_bf = keep.tile([P, 4 * H], BF16, name="w1_bf", align_bytes=64)
        w2_bf = keep.tile([P, 8 * N], BF16, name="w2_bf", align_bytes=64)
        w2_codes = keep.tile([P, 2 * N], U32, name="w2_codes", align_bytes=64)
        w2_scales = keep.tile([P, 2 * N], U8, name="w2_scales", align_bytes=64)
        h = [keep.tile([P, 2 * H], BF16, name=f"h{b}", align_bytes=64) for b in range(2)]

        def interleave(copy, dst, src):
            copy(dst.rearrange("p (c i j) -> p c j i", i=4, j=4), src.rearrange("p j (c i) -> p c j i", i=4))

        def quant(codes, scales, bf):
            nc.vector.quantize_mx(out=codes.bitcast(FP8X4), scales=scales, in_=bf)

        def cast_x(copy, b, raw, r0, c0, w):
            interleave(copy, x_bf[b][:, 4 * c0 : 4 * (c0 + w)], raw[:, :, r0 : r0 + w])

        def quant_x(b):
            quant(x_codes[b][:], x_scales[b][:], x_bf[b][:])

        def cast_w1(copy, raw, r0, c0, w):
            interleave(copy, w1_bf[:, 4 * c0 : 4 * (c0 + w)], raw[:, :, r0 : r0 + w])

        def quant_w1(c0, w):
            quant(w1_codes[:, c0 : c0 + w], w1_scales[:, c0 : c0 + w], w1_bf[:, 4 * c0 : 4 * (c0 + w)])

        def cast_w2(copy):
            copy(w2_bf[:].rearrange("p (g n j) -> p g n j", g=2, j=4), w2_raw[:].rearrange("p g j n -> p g n j"))

        def layer1(b, bank_index, c0, w):
            ps = bank(bank_index, [P, 2, w])
            ch = slice(c0, c0 + w)
            for e in range(2):
                cols = slice(e * P, (e + 1) * P)
                nc.tensor.matmul_mx(
                    out=ps[:, e, :],
                    lhsT=x_codes[b][:, cols].bitcast(FP8X4),
                    lhsT_scale=x_scales[b][:, cols],
                    rhs=w1_codes[:, ch].bitcast(FP8X4),
                    rhs_scale=w1_scales[:, ch],
                    start=True,
                    stop=True,
                )
            nc.scalar.activation(
                h[b][:, 2 * c0 : 2 * (c0 + w)].rearrange("p (c e) -> p c e", e=2),
                ps[:].rearrange("p e c -> p c e"),
                SILU,
            )

        def gather(b, g):
            gt = keep.tile([P, 4 * P * 2], BF16, name=f"gt{b}{g}", align_bytes=64)
            nc.vector.tensor_copy(
                out=gt[:].bitcast(U32).rearrange("p (t m) -> p m t", t=4),
                in_=h[b][:].bitcast(U32).indirect(offsets[:, 32 * g : 32 * (g + 1)]),
            )
            return gt

        def turn(gt, bank_index):
            pt = bank(bank_index, [P, 4, P])
            for t in range(4):
                nc.tensor.transpose(pt[:, t, :], gt[:].bitcast(F32)[:, t * P : (t + 1) * P], ident[:])
            return pt

        h_bf = {}
        h_codes = {}
        h_scales = {}

        def evac(copy, b, g, pt, e0=0, e1=2):
            if (b, g) not in h_bf:
                h_bf[b, g] = keep.tile([P, 4 * TB], BF16, name=f"h_bf{b}{g}", align_bytes=64)
                h_codes[b, g] = keep.tile([P, TB], U32, name=f"h_codes{b}{g}", align_bytes=64)
                h_scales[b, g] = keep.tile([P, TB], U8, name=f"h_scales{b}{g}", align_bytes=64)
            copy(
                h_bf[b, g][:].rearrange("p (e q t) -> p e q t", e=2, t=4)[:, e0:e1],
                pt[:].bitcast(BF16).rearrange("p t (q e) -> p e q t", e=2)[:, e0:e1],
            )

        def quant_h(b, g, e0=0, e1=2):
            cols = slice(e0 * P, e1 * P)
            quant(h_codes[b, g][:, cols], h_scales[b, g][:, cols], h_bf[b, g][:, 4 * e0 * P : 4 * e1 * P])

        def layer2(acc, b, g, e0=0, e1=2):
            cols = slice(e0 * P, e1 * P)
            nc.tensor.matmul_mx(
                out=acc[:],
                lhsT=w2_codes[:, g * N : (g + 1) * N].bitcast(FP8X4),
                lhsT_scale=w2_scales[:, g * N : (g + 1) * N],
                rhs=h_codes[b, g][:, cols].bitcast(FP8X4),
                rhs_scale=h_scales[b, g][:, cols],
                start=(g == 0),
                stop=(g == 1),
            )

        def leave(copy, acc, t0, w):
            res = keep.tile([P, w], F32, name=f"res{t0}")
            copy(res[:], acc[:])
            nc.sync.dma_start(out[:, t0 : t0 + w], res[:])

        cast_x(S, 0, x_raw[0], 0, 0, 128)
        cast_x(V, 0, x_raw[0], 128, 128, 128)
        quant_x(0)
        cast_w1(V, w1_raw[0], 0, 0, 256)
        cast_w1(S, w1_raw[0], 256, 256, 256)
        quant_w1(0, 256)
        layer1(0, 0, 0, 256)
        quant_w1(256, 256)
        layer1(0, 1, 256, 256)
        cast_w1(S, w1_raw[512], 0, 512, 256)
        cast_w1(V, w1_raw[768], 0, 768, 256)
        quant_w1(512, 256)
        layer1(0, 2, 512, 256)
        quant_w1(768, 256)
        layer1(0, 3, 768, 256)
        cast_x(V, 1, x_raw[256], 0, 0, 256)
        quant_x(1)
        layer1(1, 4, 0, 256)
        layer1(1, 5, 256, 256)
        layer1(1, 6, 512, 256)
        layer1(1, 7, 768, 256)
        cast_w2(G)
        p00 = turn(gather(0, 0), 0)
        p01 = turn(gather(0, 1), 1)
        p10 = turn(gather(1, 0), 2)
        quant(w2_codes[:], w2_scales[:], w2_bf[:])
        p11 = turn(gather(1, 1), 3)
        evac(S, 0, 0, p00, 0, 2)
        evac(S, 0, 1, p01, 0, 2)
        evac(S, 1, 0, p10, 0, 2)
        evac(S, 1, 1, p11, 0, 1)
        evac(S, 1, 1, p11, 1, 2)
        quant_h(0, 0, 0, 2)
        quant_h(0, 1, 0, 2)
        quant_h(1, 0, 0, 2)
        quant_h(1, 1, 0, 1)
        quant_h(1, 1, 1, 2)
        a00 = bank(4, [P, 256])
        layer2(a00, 0, 0, 0, 2)
        layer2(a00, 0, 1, 0, 2)
        leave(S, a00, 0, 256)
        a10 = bank(5, [P, 128])
        layer2(a10, 1, 0, 0, 1)
        layer2(a10, 1, 1, 0, 1)
        leave(S, a10, 256, 128)
        a11 = bank(6, [P, 128])
        layer2(a11, 1, 0, 1, 2)
        layer2(a11, 1, 1, 1, 2)
        leave(S, a11, 384, 128)
